import numpy as np
import ml_dtypes


def mxq(x, axis, fmt="e4m3"):
    dtype, down = {"e4m3": (ml_dtypes.float8_e4m3fn, 7), "e5m2": (ml_dtypes.float8_e5m2, 14)}[fmt]
    v = np.moveaxis(np.asarray(x, np.float32).astype(ml_dtypes.bfloat16).astype(np.float64), axis, -1)
    blocks = v.reshape(v.shape[:-1] + (-1, 32))
    amax = np.abs(blocks).max(-1, keepdims=True)
    byte = np.maximum(np.where(amax > 0, np.frexp(amax)[1] - 1 + 127, 0) - down, 1)
    scale = np.exp2(byte - 127.0)
    codes = (blocks / scale).astype(np.float32).astype(dtype).astype(np.float64)
    return np.moveaxis((codes * scale).reshape(v.shape), -1, axis)


WIDE = False


def mx_kscale(k):
    if not WIDE:
        return np.ones(k)
    levels = np.array([10, -10, 5, -5, 0])
    if k % 512:
        return np.exp2(np.random.permutation(np.resize(levels, k // 32))).repeat(32)
    a = np.empty((k // 512, 16))
    for p in range(k // 512):
        a[p, :8] = np.random.permutation(np.resize(levels, 8))
        for g in range(8):
            far = levels[np.abs(levels - a[p, g]) >= 10]
            a[p, g + 8] = far[np.random.randint(len(far))]
    return np.exp2(a.ravel()).repeat(32)


BF16 = ml_dtypes.bfloat16


def bf(x):
    return np.asarray(x, np.float32).astype(BF16)


def f64(x):
    return np.asarray(x).astype(np.float64)

def planes(Y):
    n, m = Y.shape
    b = f64(bf(Y)).reshape(n // 32, 32, m)
    amax = np.abs(b).max(1)
    byte = np.clip(np.where(amax > 0, np.frexp(amax)[1] - 1 + 127 - 7, 1), 1, 254)
    codes = (b * np.exp2(127.0 - byte)[:, None, :]).reshape(n, m).astype(np.float32).astype(ml_dtypes.float8_e4m3fn).view(np.uint8)
    words = codes.reshape(n // 512, 128, 4, m).transpose(0, 1, 3, 2)
    return np.ascontiguousarray(words), np.ascontiguousarray(byte.astype(np.uint8).reshape(n // 512, 16, m))


M, K, N = 1024, 4096, 1024

FMT = "e4m3"


def setup_inputs():
    s = mx_kscale(K)
    z = bf(np.random.randn(M, K))
    theta = bf(0.2 + 0.2 * np.random.randn(K))
    g = bf((1.0 + 0.1 * np.random.randn(K)) * s)
    D = bf(1.5 * np.random.randn(K, N) / np.sqrt(K) / s[:, None])
    b = bf(0.4 * np.random.randn(N))
    sigma = bf(np.exp(0.8 * np.random.randn(N)))
    rho = bf(np.exp(0.3 * np.random.randn(M)))
    return {"z": z, "theta": theta, "g": g, "D": D, "b": b, "sigma": sigma, "rho": rho}


def reference(z, theta, g, D, b, sigma, rho):
    c = np.maximum(f64(z) - f64(theta), 0.0) * f64(g)
    p = mxq(c, 1, FMT) @ mxq(f64(D), 0, FMT)
    y = (p + f64(b)) * f64(sigma) * f64(rho)[:, None]
    Y = y.reshape(M, N).T
    words, scales = planes(Y)
    return y, words, scales

@@ -1,0 +1,436 @@
+from contextlib import ExitStack
+
+import concourse.mybir as mybir
+from concourse.masks import make_identity
+
+M, K, N = 1024, 4096, 1024
+FLOPS = 2 * M * K * N
+
+F32 = mybir.dt.float32
+BF16 = mybir.dt.bfloat16
+U32 = mybir.dt.uint32
+I32 = mybir.dt.int32
+U8 = mybir.dt.uint8
+FP8X4 = mybir.dt.float8_e4m3fn_x4
+ALU = mybir.AluOpType
+ACT = mybir.ActivationFunctionType
+
+P = 128
+PACK = 4
+KP = P * PACK
+PASSES = K // KP
+W = 512
+RAW_BUFS = 6
+D_BUFS = 8
+CT_BUFS = 3
+GROUP_BUFS = 2
+OUT_BUFS = 4
+SPLIT_LOAD = ()
+LEAD = 3
+STREAMED = 2
+TAIL = ((0, 256), (256, 256))
+TAIL_BANKS = (2, 3)
+TURNS = (2, 3, 5, 6)
+EXTRA_TURN = (6, 9)
+FILL = (0, 1, 2, 3, 4, 5, 6)
+Y_AT = 14
+A_DRAIN = 4
+VORD = 1
+FIRST_10 = 6
+RUNS_FROM = 7
+V_SIGN = (5, 6)
+SIGN_ON_C = ()
+SCALAR_D = ((1, 1), (2, 1), (3, 1), (4, 1), (5, 1), (6, 1), (7, 1), (9, 0), (9, 1), (10, 1), (11, 1), (12, 1), (13, 1), (14, 1), (15, 1))
+VECTOR_DRAIN = ((0, 0, 0, 2), (0, 0, 0, 3))
+VECTOR_FINISH = ()
+
+
+def tile_dictionary_relu_readout_g1_kernel(tc, z, theta, g, D, b, sigma, rho, out_0, out_1, out_2):
+    nc = tc.nc
+    with ExitStack() as ctx:
+        sb = ctx.enter_context(tc.tile_pool(name="sb", bufs=1))
+        ps = ctx.enter_context(tc.psum_pool(name="ps", bufs=1))
+        ctx.enter_context(tc.manual_schedule())
+        tl = {}
+
+        def bank(i, dtype=F32, width=W):
+            return ps.tile([P, width], dtype, name="bank%d" % i, tag="bank%d" % i)
+
+        def stile(key, shape, dtype, slot):
+            tl[key] = sb.tile(shape, dtype, name="%s%s" % (key[0], slot), tag="%s%s" % (key[0], slot), align_bytes=64)
+            return tl[key]
+
+        ident = sb.tile([P, P], F32, name="ident")
+        ident_bf = sb.tile([P, P], BF16, name="ident_bf")
+        stage = sb.tile([P, W], BF16, name="stage")
+        par = sb.tile([P, 20, PACK], F32, name="par")
+        abs_g = sb.tile([P, 32], F32, name="abs_g")
+        neg_bias = sb.tile([P, 32], F32, name="neg_bias")
+        sign_g = sb.tile([P, 32], F32, name="sign_g")
+        sigma_b = sb.tile([P, 8], F32, name="sigma_b")
+        rho_col = sb.tile([P, 8], F32, name="rho_col")
+        rho_row = sb.tile([P, M], BF16, name="rho_row")
+        warm = sb.tile([P, 8], F32, name="warm")
+        y_scales = [sb.tile([P, M], U8, name="y_scales%d" % i, align_bytes=64) for i in range(2)]
+        flat = par[:].rearrange("p r t -> p (r t)")
+
+        def head():
+            nc.vector.memset(stage[:].bitcast(U32), 0)
+            nc.vector.memset(warm[:], 0.0)
+            nc.scalar.dma_start(out=stage[0:8, :], in_=theta.rearrange("(r c) -> r c", c=W))
+            nc.scalar.dma_start(out=stage[8:16, :], in_=g.rearrange("(r c) -> r c", c=W))
+            nc.scalar.dma_start(out=stage[16:18, :], in_=b.rearrange("(r c) -> r c", c=W))
+            nc.scalar.dma_start(out=stage[18:20, :], in_=sigma.rearrange("(r c) -> r c", c=W))
+            nc.scalar.dma_start(out=stage[20:28, 0:P], in_=rho.rearrange("(r c) -> r c", c=P))
+            nc.scalar.activation(out=warm[:, 0:1], in_=warm[:, 1:2], func=ACT.Relu)
+            make_identity(nc, ident[:])
+            make_identity(nc, ident_bf[:])
+
+        def turn_constants():
+            words = stage[:].bitcast(F32)
+            pt = bank(0)
+            tl["pt"] = pt
+            for u in range(2):
+                nc.tensor.transpose(pt[:, u * P:(u + 1) * P], words[:, u:256:2], ident[:])
+
+        def turn_rho():
+            pr = bank(1, BF16, 2 * W)
+            tl["pr"] = pr
+            nc.tensor.transpose(pr[:, 0:P], stage[:, 0:P], ident_bf[:])
+
+        def relu_constants():
+            halves = tl["pt"][:].bitcast(BF16)[:, 0:4 * P].rearrange("p (u r e) -> p r u e", u=2, e=2)
+            nc.vector.tensor_copy(out=par[:].rearrange("p r (u e) -> p r u e", e=2), in_=halves[:, 0:20, :, :])
+            nc.vector.scalar_tensor_tensor(out=abs_g[:], in0=flat[:, 32:64], scalar=-1.0, in1=flat[:, 32:64],
+                                           op0=ALU.mult, op1=ALU.max)
+            nc.vector.tensor_scalar(out=sign_g[:], in0=flat[:, 32:64], scalar1=0.0, scalar2=2.0,
+                                    op0=ALU.is_ge, op1=ALU.mult)
+            nc.vector.scalar_tensor_tensor(out=neg_bias[:], in0=flat[:, 0:32], scalar=-1.0, in1=abs_g[:],
+                                           op0=ALU.mult, op1=ALU.mult)
+            nc.vector.tensor_scalar(out=sign_g[:], in0=sign_g[:], scalar1=-1.0, scalar2=None, op0=ALU.add)
+
+        def late_constants():
+            nc.vector.tensor_tensor(out=sigma_b[:], in0=flat[:, 64:72], in1=flat[:, 72:80], op=ALU.mult)
+            nc.vector.tensor_copy(out=rho_col[:], in_=tl["pr"][:, 20:28])
+
+        def load_z(i):
+            h, k = divmod(i, PASSES)
+            raw = stile(("zraw", i), [P, 4, KP], BF16, i % RAW_BUFS)
+            nc.sync.dma_start(out=raw[:], in_=z[h * W:(h + 1) * W, k * KP:(k + 1) * KP].rearrange("(a p) k -> p a k", p=P))
+
+        def load_d(i, part):
+            gi, k = divmod(i, PASSES)
+            if ("draw", i) not in tl:
+                stile(("draw", i), [P, PACK, W], BF16, i % D_BUFS)
+            cut = (slice(0, W // 2), slice(W // 2, W), slice(0, W))[part]
+            rows = D[k * KP:(k + 1) * KP, gi * W:(gi + 1) * W].rearrange("(p j) n -> p j n", j=PACK)
+            nc.sync.dma_start(out=tl[("draw", i)][:, :, cut], in_=rows[:, :, cut])
+
+        def loads(i):
+            return [(load_d, i, 0), (load_d, i, 1)] if i in SPLIT_LOAD else [(load_d, i, 2)]
+
+        def load_rho():
+            nc.sync.dma_start(out=rho_row[:], in_=rho.partition_broadcast(P))
+
+        def turn_z(i, u):
+            tb = bank(4 + (2 * i + u) % 4)
+            tl[("zt", i, u)] = tb
+            for a in range(4):
+                words = tl[("zraw", i)][:, a, :].bitcast(F32)
+                nc.tensor.transpose(tb[:, a * P:(a + 1) * P], words[:, u:256:2], ident[:])
+
+        def relu_z(i, u):
+            if u == 0:
+                stile(("ct", i), [P, PACK, W], BF16, i % CT_BUFS)
+            halves = tl[("zt", i, u)][:].bitcast(BF16)
+            for e in range(2):
+                t = 2 * u + e
+                col = PACK * (i % PASSES) + t
+                nc.scalar.activation(out=tl[("ct", i)][:, t, :], in_=halves[:, e:2 * W:2], func=ACT.Relu,
+                                     bias=neg_bias[:, col:col + 1], scale=abs_g[:, col:col + 1])
+
+        def weave_z(i):
+            dst = stile(("cg", i), [P, PACK * W], BF16, i % GROUP_BUFS)
+            nc.vector.tensor_copy(out=dst[:].rearrange("p (c i t) -> p c t i", i=4, t=PACK),
+                                  in_=tl[("ct", i)][:].rearrange("p t (c i) -> p c t i", i=4))
+
+        def quant(kind, i):
+            codes = stile((kind + "codes", i), [P, W], U32, i)
+            scales = stile((kind + "scales", i), [P, W], U8, i)
+            nc.vector.quantize_mx(out=codes[:].bitcast(FP8X4), scales=scales[:], in_=tl[(kind + "g", i)][:])
+
+        def sign(kind, i):
+            raw = tl[(kind, i)]
+            for j in range(PACK):
+                col = PACK * (i % PASSES) + j
+                nc.vector.tensor_scalar(out=raw[:, j, :], in0=raw[:, j, :], scalar1=sign_g[:, col:col + 1],
+                                        scalar2=None, op0=ALU.mult)
+
+        def weave_d(i, part):
+            if ("dg", i) not in tl:
+                stile(("dg", i), [P, PACK * W], BF16, i % (GROUP_BUFS + 1))
+            cut = (slice(0, 64), slice(64, 128), slice(0, 128))[part]
+            dst = tl[("dg", i)][:].rearrange("p (t m j) -> p m j t", t=4, j=PACK)[:, cut]
+            src = tl[("draw", i)][:].rearrange("p j (m t) -> p m j t", t=4)[:, cut]
+            if (i, part) in SCALAR_D:
+                nc.scalar.copy(out=dst, in_=src)
+            else:
+                nc.vector.tensor_copy(out=dst, in_=src)
+
+        def weaves(i):
+            split = (i, 0) in SCALAR_D or (i, 1) in SCALAR_D
+            return [(weave_d, i, 0), (weave_d, i, 1)] if split else [(weave_d, i, 2)]
+
+        def multiply(gi, h, lo, wd, k, t, bk):
+            if k == 0:
+                tl[("acc", gi, h, lo, t)] = bank(bk)
+            di, zi = gi * PASSES + k, h * PASSES + k
+            nc.tensor.matmul_mx(
+                out=tl[("acc", gi, h, lo, t)][:, 0:wd],
+                lhsT=tl[("dcodes", di)][:, t * P:(t + 1) * P].bitcast(FP8X4),
+                lhsT_scale=tl[("dscales", di)][:, t * P:(t + 1) * P],
+                rhs=tl[("ccodes", zi)][:, lo:lo + wd].bitcast(FP8X4),
+                rhs_scale=tl[("cscales", zi)][:, lo:lo + wd],
+                start=(k == 0), stop=(k == PASSES - 1))
+
+        def drain(gi, h, lo, wd, t):
+            if ("w", gi, h) not in tl:
+                stile(("w", gi, h), [P, PACK, W], F32, 2 * gi + h)
+            col = PACK * gi + t
+            dst, src = tl[("w", gi, h)][:, t, lo:lo + wd], tl[("acc", gi, h, lo, t)][:, 0:wd]
+            bias, scale = sigma_b[:, col:col + 1], flat[:, 72 + col:73 + col]
+            if (gi, h, lo, t) in VECTOR_DRAIN:
+                nc.vector.tensor_scalar(out=dst, in0=src, scalar1=scale, scalar2=bias, op0=ALU.mult, op1=ALU.add)
+            else:
+                nc.scalar.activation(out=dst, in_=src, func=ACT.Identity, bias=bias, scale=scale)
+
+        def weave_y(gi, h, lo, wd):
+            dst = stile(("yg", gi, h, lo), [P, PACK * wd], BF16, pieces.index((gi, h, lo, wd)) % 2)
+            factor = rho_row[:, h * W + lo:h * W + lo + wd].rearrange("p (c i) -> p c i", i=4)
+            nc.vector.tensor_tensor(
+                out=dst[:].rearrange("p (c i t) -> p c t i", i=4, t=PACK),
+                in0=tl[("w", gi, h)][:, :, lo:lo + wd].rearrange("p t (c i) -> p c t i", i=4),
+                in1=factor.unsqueeze(2).to_broadcast([P, wd // 4, PACK, 4]), op=ALU.mult)
+
+        def quant_y(gi, h, lo, wd):
+            codes = stile(("ycodes", gi, h, lo), [P, wd], U32, pieces.index((gi, h, lo, wd)) % 2)
+            m0 = h * W + lo
+            nc.vector.quantize_mx(out=codes[:].bitcast(FP8X4), scales=y_scales[gi][:, m0:m0 + wd],
+                                  in_=tl[("yg", gi, h, lo)][:])
+
+        def store_words(gi, h, lo, wd):
+            m0 = h * W + lo
+            nc.sync.dma_start(out=out_1[gi, :, m0:m0 + wd, :].rearrange("p m t -> p (m t)").bitcast(I32),
+                              in_=tl[("ycodes", gi, h, lo)][:].bitcast(I32))
+
+        def store_scales(gi):
+            for q in range(4):
+                nc.sync.dma_start(out=out_2[gi, 4 * q:4 * q + 4, :].bitcast(I32),
+                                  in_=y_scales[gi][32 * q:32 * q + 4, :].bitcast(I32))
+
+        def turn_w(gi, h, a, bk):
+            tb = bank(bk)
+            tl[("wt", gi, h, a)] = tb
+            for t in range(PACK):
+                nc.tensor.transpose(tb[:, t * P:(t + 1) * P], tl[("w", gi, h)][:, t, a * P:(a + 1) * P], ident[:])
+
+        def finish(gi, h, a):
+            yo = stile(("yo", gi, h, a), [P, W], F32, (8 * gi + 4 * h + a) % OUT_BUFS)
+            dst = yo[:].rearrange("m (p t) -> m p t", t=PACK)
+            src = tl[("wt", gi, h, a)][:].rearrange("m (t p) -> m p t", t=PACK)
+            scale = rho_col[:, 4 * h + a:4 * h + a + 1]
+            if (gi, h, a) in VECTOR_FINISH:
+                nc.vector.tensor_scalar(out=dst, in0=src, scalar1=scale, scalar2=None, op0=ALU.mult)
+            else:
+                nc.scalar.activation(out=dst, in_=src, func=ACT.Copy, scale=scale)
+
+        def store_y(gi, h, a):
+            m0 = h * W + a * P
+            nc.sync.dma_start(out=out_0[m0:m0 + P, gi * W:(gi + 1) * W], in_=tl[("yo", gi, h, a)][:])
+
+        def covering(gi, h, lo, wd):
+            return [s for s in scalar + vector if s[0] is drain and s[1:3] == (gi, h) and s[3] < lo + wd and lo < s[3] + s[4]]
+
+        def needs(step):
+            f, a = step[0], step[1:]
+            if f is load_z:
+                return [(turn_z, a[0] - RAW_BUFS, 1)] if a[0] >= RAW_BUFS else []
+            if f is load_d:
+                j = a[0] - D_BUFS
+                return weaves(j) if j >= 0 else []
+            if f is relu_constants:
+                return [(turn_constants,)]
+            if f is late_constants:
+                return [(turn_rho,), (relu_constants,)]
+            if f is turn_z:
+                return [(load_z, a[0])] + freed[step]
+            if f is relu_z:
+                return [(turn_z, a[0], a[1]), (relu_constants,)] + ([(weave_z, a[0] - CT_BUFS)] if a[0] >= CT_BUFS else [])
+            if f is weave_z:
+                r = [(sign, "ct", a[0])] if a[0] % PASSES in SIGN_ON_C else [(relu_z, a[0], 1)]
+                return r + ([(quant, "c", a[0] - GROUP_BUFS)] if a[0] >= GROUP_BUFS else [])
+            if f is sign:
+                return loads(a[1]) + [(relu_constants,)] if a[0] == "draw" else [(relu_z, a[1], 1)]
+            if f is weave_d:
+                j = a[0] - GROUP_BUFS - 1
+                r = [x for x in loads(a[0]) if 2 in (x[2], a[1]) or x[2] == a[1]] if a[0] % PASSES in SIGN_ON_C else [(sign, "draw", a[0])]
+                return r + ([(quant, "d", j)] if j >= 0 else [])
+            if f is quant:
+                if a[0] == "c":
+                    return [(weave_z, a[1])]
+                return weaves(a[1])
+            if f is multiply:
+                gi, h, lo, wd, k, t, bk = a
+                r = [(quant, "d", gi * PASSES + k), (quant, "c", h * PASSES + k)]
+                return r + (freed[step] if k == 0 else [(multiply, gi, h, lo, wd, k - 1, t, bk)])
+            if f is drain:
+                return [last_pass[a], (late_constants,)]
+            if f is weave_y:
+                n = pieces.index(a)
+                return covering(*a) + [(load_rho,)] + ([(quant_y,) + pieces[n - 2]] if n >= 2 else [])
+            if f is quant_y:
+                n = pieces.index(a)
+                return [(weave_y,) + a] + ([(store_words,) + pieces[n - 2]] if n >= 2 else [])
+            if f is store_words:
+                return [(quant_y,) + a]
+            if f is store_scales:
+                return [s for s in vector if s[0] is quant_y and s[1] == a[0]]
+            if f is turn_w:
+                gi, h, at, bk = a
+                return covering(gi, h, at * P, P) + freed[step]
+            if f is finish:
+                n = outs.index(a)
+                r = [s for s in tensor if s[0] is turn_w and s[1:4] == a]
+                return r + ([(store_y,) + outs[n - OUT_BUFS]] if n >= OUT_BUFS else [])
+            if f is store_y:
+                return [(finish,) + a]
+            return []
+
+        H = W // 2
+        pieces = [(0, 0, 0, W), (0, 1, 0, W), (1, 0, 0, W)] + [(1, 1) + x for x in TAIL]
+        rest = range(STREAMED, 4)
+        groups = [(lo, wd, t) for lo, wd in TAIL for t in rest]
+        outs = [(gi, h, a) for gi in range(2) for h in range(2) for a in range(4)]
+        tensor, scalar, vector, sync = [], [], [], []
+        L = PASSES
+
+        def passes(gi, h, k, ts, first_bank):
+            return [(multiply, gi, h, 0, W, k, t, first_bank + t) for t in ts]
+
+        def turns(n0, n1, banks):
+            return [(turn_w,) + outs[n] + (banks[n % len(banks)],) for n in range(n0, n1)]
+
+        def finishes(n0, n1):
+            return [(finish,) + outs[n] for n in range(n0, n1)]
+
+        def stores(n0, n1):
+            return [(store_y,) + outs[n] for n in range(n0, n1)]
+
+        one = range(L)
+
+        def relus(i):
+            return [(relu_z, i, 0), (relu_z, i, 1)]
+
+        def drains(gi, h, ts):
+            return [(drain, gi, h, 0, W, t) for t in ts]
+
+        def group(n):
+            lo, wd, t = groups[n]
+            return [(multiply, 1, 1, lo, wd, k, t, TAIL_BANKS[n % len(TAIL_BANKS)]) for k in one]
+
+        def tail_drain(n):
+            return [(drain, 1, 1) + groups[n]]
+
+        def words(n):
+            return [(store_words,) + pieces[n]]
+
+        sync += [(load_z, 0)]
+        for k in range(L - 1):
+            sync += [(load_d, k, 2)] * (k == 0) + [(load_d, k + 1, 2), (load_z, k + 1)]
+        for k in one:
+            sync += [(load_z, L + k), (load_d, L + k, 2)]
+        sync += [(load_rho,)]
+        sync += stores(0, 8) + words(0) + words(1) + [(store_scales, 0)]
+        sync += stores(8, 10) + words(2) + stores(10, 13) + words(3) + stores(13, 16) + words(4) + [(store_scales, 1)]
+
+        tensor += [(turn_constants,), (turn_z, 0, 0), (turn_z, 0, 1), (turn_rho,)]
+        tensor += [(turn_z, i, u) for i in range(1, LEAD) for u in range(2)]
+        ahead = [(turn_z, i, u) for i in range(LEAD, 2 * L) for u in range(2)]
+        for k in range(2 * L):
+            h, j = divmod(k, L)
+            early = ahead[0:EXTRA_TURN.count(k)]
+            ahead = ahead[len(early):]
+            if k >= RUNS_FROM:
+                tensor += early + passes(0, h, j, range(4), 0) + ahead[0:2]
+            else:
+                tensor += early + passes(0, h, j, (0, 1), 0) + ahead[0:1] + passes(0, h, j, (2, 3), 0) + ahead[1:2]
+            ahead = ahead[2:]
+            if k == L + FIRST_10:
+                tensor += passes(1, 0, 0, range(4), 4)
+        for k in one:
+            tensor += passes(1, 0, k, range(4), 4) if k > 0 else []
+            if k in TURNS:
+                n = 2 * TURNS.index(k)
+                tensor += turns(n, n + 2, (2, 3))
+            if k > 0:
+                tensor += passes(1, 1, k - 1, (0, 1), 0)
+        tensor += passes(1, 1, L - 1, (0, 1), 0)
+        tensor += group(0) + turns(8, 10, (4, 5)) + group(1) + turns(10, 12, (6, 7)) + group(2) + turns(12, 14, (0, 1))
+        tensor += group(3) + turns(14, 16, (4, 5))
+
+        for k in one:
+            scalar += relus(k) + ([(weave_d, k + 1, 1)] if k + 1 < L else [])
+        second = [x for k in one for x in relus(L + k)]
+        scalar += second[:A_DRAIN] + drains(0, 0, (0, 1)) + second[A_DRAIN:]
+        scalar += [(weave_d, 9, 0), (weave_d, 9, 1), (weave_d, 10, 1)] + drains(0, 1, range(4))
+        scalar += [(weave_d, 11, 1)] + finishes(0, 1) + [(weave_d, 12, 1)] + finishes(1, 2) + [(weave_d, 13, 1)] + finishes(2, 4)
+        scalar += [(weave_d, 14, 1), (weave_d, 15, 1)] + finishes(4, 8)
+        scalar += drains(1, 0, range(4)) + drains(1, 1, (0,)) + finishes(8, 9) + tail_drain(0) + drains(1, 1, (1,)) + finishes(9, 10)
+        scalar += tail_drain(1) + finishes(10, 12) + tail_drain(2) + finishes(12, 14) + tail_drain(3) + finishes(14, 16)
+
+        vector += [(relu_constants,), (sign, "draw", 0), (weave_d, 0, 2), (sign, "draw", 1), (quant, "d", 0), (weave_d, 1, 0), (late_constants,)]
+        for k in range(L - 2):
+            vector += [(weave_z, k), (sign, "draw", k + 2), (quant, "c", k), (weave_d, k + 2, 0), (quant, "d", k + 1)]
+        vector += [(weave_z, L - 2), (quant, "d", L - 1), (quant, "c", L - 2), (weave_z, L - 1), (sign, "draw", L), (quant, "c", L - 1)]
+        fill = [x for x in drains(0, 0, range(4)) if x[1:4] + x[5:] in VECTOR_DRAIN]
+        vector += [[(weave_z, L)] + fill[0:1] + [(quant, "c", L)] + fill[1:2] + [(sign, "draw", 9)],
+                   [(weave_z, L), (sign, "draw", 9), (quant, "c", L)] + fill,
+                   [(weave_z, L)] + fill + [(quant, "c", L), (sign, "draw", 9)]][VORD]
+        vector += [(weave_z, 9), (weave_d, 8, 2), (quant, "c", 9), (weave_z, 10), (quant, "d", 8), (quant, "c", 10)]
+        vector += [(weave_z, 11), (weave_z, 12), (quant, "c", 11), (quant, "c", 12), (weave_z, 13), (quant, "c", 13)]
+        vector += [(weave_z, 14), (quant, "c", 14), (weave_z, 15), (sign, "draw", 10), (quant, "c", 15), (quant, "d", 9)]
+        for i in range(10, 2 * L - 1):
+            vector += [(weave_d, i, 0), (sign, "draw", i + 1), (quant, "d", i)]
+        vector += [(weave_d, 15, 0), (weave_y,) + pieces[0], (quant, "d", 15), (weave_y,) + pieces[1], (quant_y,) + pieces[0], (quant_y,) + pieces[1]]
+        for n in range(2, 5):
+            vector += [(weave_y,) + pieces[n], (quant_y,) + pieces[n]]
+
+        freed, last_pass, holder = {}, {}, {0: (relu_constants,), 1: (late_constants,)}
+        for s in tensor:
+            if s[0] is turn_z:
+                bk = 4 + (2 * s[1] + s[2]) % 4
+                freed[s] = [holder[bk]] if bk in holder else []
+                holder[bk] = (relu_z, s[1], s[2])
+            elif s[0] is multiply:
+                if s[5] == 0:
+                    freed[s] = [holder[s[7]]] if s[7] in holder else []
+                    holder[s[7]] = (drain,) + s[1:5] + (s[6],)
+                last_pass[s[1:5] + (s[6],)] = s
+            elif s[0] is turn_w:
+                freed[s] = [holder[s[4]]]
+                holder[s[4]] = (finish,) + s[1:4]
+
+        head()
+        written = set()
+        queues = [sync, tensor, scalar, vector]
+        places = [0, 0, 0, 0]
+        while any(places[e] < len(queues[e]) for e in range(4)):
+            moved = False
+            for e in range(4):
+                while places[e] < len(queues[e]) and all(s in written for s in needs(queues[e][places[e]])):
+                    step = queues[e][places[e]]
+                    step[0](*step[1:])
+                    written.add(step)
+                    places[e] += 1
+                    moved = True
+            assert moved

@@ -17,32 +17,28 @@ ACT = mybir.ActivationFunctionType
 
 P = 128
 PACK = 4
-KP = P * PACK
-PASSES = K // KP
+K_PASS = P * PACK
+PASSES = K // K_PASS
+UNITS = 2 * PASSES
 W = 512
-RAW_BUFS = 6
+SUBTILES = W // P
+
+Z_BUFS = 6
 D_BUFS = 8
-CT_BUFS = 3
-GROUP_BUFS = 2
+RELU_BUFS = 3
+WOVEN_BUFS = {"c": 2, "d": 3}
+PLANE_BUFS = 2
 OUT_BUFS = 4
-SPLIT_LOAD = ()
+
+THETA_ROW, G_ROW, B_ROW, SIGMA_ROW, RHO_ROW = 0, 8, 16, 18, 20
+
+FIRST, SECOND, WHOLE = 0, 1, 2
+
+LOW, HIGH = 0, 4
 LEAD = 3
-STREAMED = 2
-TAIL = ((0, 256), (256, 256))
-TAIL_BANKS = (2, 3)
-TURNS = (2, 3, 5, 6)
 EXTRA_TURN = (6, 9)
-FILL = (0, 1, 2, 3, 4, 5, 6)
-Y_AT = 14
-A_DRAIN = 4
-VORD = 1
-FIRST_10 = 6
-RUNS_FROM = 7
-V_SIGN = (5, 6)
-SIGN_ON_C = ()
-SCALAR_D = ((1, 1), (2, 1), (3, 1), (4, 1), (5, 1), (6, 1), (7, 1), (9, 0), (9, 1), (10, 1), (11, 1), (12, 1), (13, 1), (14, 1), (15, 1))
-VECTOR_DRAIN = ((0, 0, 0, 2), (0, 0, 0, 3))
-VECTOR_FINISH = ()
+TURN_AFTER = (2, 3, 5, 6)
+PIECES_11 = ((0, 256), (256, 128), (384, 128))
 
 
 def tile_dictionary_relu_readout_g1_kernel(tc, z, theta, g, D, b, sigma, rho, out_0, out_1, out_2):
@@ -51,386 +47,368 @@ def tile_dictionary_relu_readout_g1_kernel(tc, z, theta, g, D, b, sigma, rho, ou
         sb = ctx.enter_context(tc.tile_pool(name="sb", bufs=1))
         ps = ctx.enter_context(tc.psum_pool(name="ps", bufs=1))
         ctx.enter_context(tc.manual_schedule())
-        tl = {}
+        tiles = {}
 
-        def bank(i, dtype=F32, width=W):
-            return ps.tile([P, width], dtype, name="bank%d" % i, tag="bank%d" % i)
+        def bank(bank_number, dtype=F32, width=W):
+            name = "bank%d" % bank_number
+            return ps.tile([P, width], dtype, name=name, tag=name)
 
-        def stile(key, shape, dtype, slot):
-            tl[key] = sb.tile(shape, dtype, name="%s%s" % (key[0], slot), tag="%s%s" % (key[0], slot), align_bytes=64)
-            return tl[key]
+        def buffer(key, shape, dtype, slot):
+            name = "%s%d" % (key[0], slot)
+            tiles[key] = sb.tile(shape, dtype, name=name, tag=name, align_bytes=64)
+            return tiles[key]
 
         ident = sb.tile([P, P], F32, name="ident")
         ident_bf = sb.tile([P, P], BF16, name="ident_bf")
         stage = sb.tile([P, W], BF16, name="stage")
-        par = sb.tile([P, 20, PACK], F32, name="par")
-        abs_g = sb.tile([P, 32], F32, name="abs_g")
-        neg_bias = sb.tile([P, 32], F32, name="neg_bias")
-        sign_g = sb.tile([P, 32], F32, name="sign_g")
-        sigma_b = sb.tile([P, 8], F32, name="sigma_b")
-        rho_col = sb.tile([P, 8], F32, name="rho_col")
+        vectors = sb.tile([P, RHO_ROW * PACK], F32, name="vectors")
+        theta_k = vectors[:, PACK * THETA_ROW:PACK * G_ROW]
+        g_k = vectors[:, PACK * G_ROW:PACK * B_ROW]
+        b_f = vectors[:, PACK * B_ROW:PACK * SIGMA_ROW]
+        sigma_f = vectors[:, PACK * SIGMA_ROW:PACK * RHO_ROW]
+        abs_g = sb.tile([P, PACK * PASSES], F32, name="abs_g")
+        relu_bias = sb.tile([P, PACK * PASSES], F32, name="relu_bias")
+        sign_g = sb.tile([P, PACK * PASSES], F32, name="sign_g")
+        sigma_b = sb.tile([P, 2 * PACK], F32, name="sigma_b")
+        rho_col = sb.tile([P, M // P], F32, name="rho_col")
         rho_row = sb.tile([P, M], BF16, name="rho_row")
-        warm = sb.tile([P, 8], F32, name="warm")
-        y_scales = [sb.tile([P, M], U8, name="y_scales%d" % i, align_bytes=64) for i in range(2)]
-        flat = par[:].rearrange("p r t -> p (r t)")
+        codes = {"c": sb.tile([P, UNITS, W], U32, name="c_codes", align_bytes=256),
+                 "d": sb.tile([P, UNITS, W], U32, name="d_codes", align_bytes=256)}
+        scales = {"c": sb.tile([P, UNITS, W], U8, name="c_scales", align_bytes=256),
+                  "d": sb.tile([P, UNITS, W], U8, name="d_scales", align_bytes=256)}
+        y_scales = [sb.tile([P, M], U8, name="y_scales%d" % grp, align_bytes=64) for grp in range(2)]
 
-        def head():
+        def stage_vectors():
             nc.vector.memset(stage[:].bitcast(U32), 0)
-            nc.vector.memset(warm[:], 0.0)
-            nc.scalar.dma_start(out=stage[0:8, :], in_=theta.rearrange("(r c) -> r c", c=W))
-            nc.scalar.dma_start(out=stage[8:16, :], in_=g.rearrange("(r c) -> r c", c=W))
-            nc.scalar.dma_start(out=stage[16:18, :], in_=b.rearrange("(r c) -> r c", c=W))
-            nc.scalar.dma_start(out=stage[18:20, :], in_=sigma.rearrange("(r c) -> r c", c=W))
-            nc.scalar.dma_start(out=stage[20:28, 0:P], in_=rho.rearrange("(r c) -> r c", c=P))
-            nc.scalar.activation(out=warm[:, 0:1], in_=warm[:, 1:2], func=ACT.Relu)
+            for row, vec, width in ((THETA_ROW, theta, W), (G_ROW, g, W), (B_ROW, b, W), (SIGMA_ROW, sigma, W),
+                                    (RHO_ROW, rho, P)):
+                rows = vec.rearrange("(r c) -> r c", c=width)
+                nc.scalar.dma_start(out=stage[row:row + rows.shape[0], 0:width], in_=rows)
             make_identity(nc, ident[:])
-            make_identity(nc, ident_bf[:])
+            nc.scalar.activation(out=ident_bf[:], in_=ident[:], func=ACT.Relu)
 
-        def turn_constants():
+        def turn_vectors():
+            tiles["vectors_t"] = bank(LOW)
             words = stage[:].bitcast(F32)
-            pt = bank(0)
-            tl["pt"] = pt
             for u in range(2):
-                nc.tensor.transpose(pt[:, u * P:(u + 1) * P], words[:, u:256:2], ident[:])
+                nc.tensor.transpose(tiles["vectors_t"][:, u * P:(u + 1) * P], words[:, u:W // 2:2], ident[:])
 
         def turn_rho():
-            pr = bank(1, BF16, 2 * W)
-            tl["pr"] = pr
-            nc.tensor.transpose(pr[:, 0:P], stage[:, 0:P], ident_bf[:])
+            tiles["rho_t"] = bank(LOW + 1, BF16, 2 * W)
+            nc.tensor.transpose(tiles["rho_t"][:, 0:P], stage[:, 0:P], ident_bf[:])
 
-        def relu_constants():
-            halves = tl["pt"][:].bitcast(BF16)[:, 0:4 * P].rearrange("p (u r e) -> p r u e", u=2, e=2)
-            nc.vector.tensor_copy(out=par[:].rearrange("p r (u e) -> p r u e", e=2), in_=halves[:, 0:20, :, :])
-            nc.vector.scalar_tensor_tensor(out=abs_g[:], in0=flat[:, 32:64], scalar=-1.0, in1=flat[:, 32:64],
-                                           op0=ALU.mult, op1=ALU.max)
-            nc.vector.tensor_scalar(out=sign_g[:], in0=flat[:, 32:64], scalar1=0.0, scalar2=2.0,
-                                    op0=ALU.is_ge, op1=ALU.mult)
-            nc.vector.scalar_tensor_tensor(out=neg_bias[:], in0=flat[:, 0:32], scalar=-1.0, in1=abs_g[:],
+        def relu_factors():
+            halves = tiles["vectors_t"][:].bitcast(BF16)[:, 0:4 * P].rearrange("p (u r e) -> p r u e", u=2, e=2)
+            nc.vector.tensor_copy(out=vectors[:].rearrange("p (r u e) -> p r u e", u=2, e=2),
+                                  in_=halves[:, 0:RHO_ROW, :, :])
+            nc.vector.scalar_tensor_tensor(out=abs_g[:], in0=g_k, scalar=-1.0, in1=g_k, op0=ALU.mult, op1=ALU.max)
+            nc.vector.tensor_scalar(out=sign_g[:], in0=g_k, scalar1=0.0, scalar2=2.0, op0=ALU.is_ge, op1=ALU.mult)
+            nc.vector.scalar_tensor_tensor(out=relu_bias[:], in0=theta_k, scalar=-1.0, in1=abs_g[:],
                                            op0=ALU.mult, op1=ALU.mult)
             nc.vector.tensor_scalar(out=sign_g[:], in0=sign_g[:], scalar1=-1.0, scalar2=None, op0=ALU.add)
 
-        def late_constants():
-            nc.vector.tensor_tensor(out=sigma_b[:], in0=flat[:, 64:72], in1=flat[:, 72:80], op=ALU.mult)
-            nc.vector.tensor_copy(out=rho_col[:], in_=tl["pr"][:, 20:28])
+        def result_factors():
+            nc.vector.tensor_tensor(out=sigma_b[:], in0=b_f, in1=sigma_f, op=ALU.mult)
+            nc.vector.tensor_copy(out=rho_col[:], in_=tiles["rho_t"][:, RHO_ROW:RHO_ROW + M // P])
 
-        def load_z(i):
-            h, k = divmod(i, PASSES)
-            raw = stile(("zraw", i), [P, 4, KP], BF16, i % RAW_BUFS)
-            nc.sync.dma_start(out=raw[:], in_=z[h * W:(h + 1) * W, k * KP:(k + 1) * KP].rearrange("(a p) k -> p a k", p=P))
-
-        def load_d(i, part):
-            gi, k = divmod(i, PASSES)
-            if ("draw", i) not in tl:
-                stile(("draw", i), [P, PACK, W], BF16, i % D_BUFS)
-            cut = (slice(0, W // 2), slice(W // 2, W), slice(0, W))[part]
-            rows = D[k * KP:(k + 1) * KP, gi * W:(gi + 1) * W].rearrange("(p j) n -> p j n", j=PACK)
-            nc.sync.dma_start(out=tl[("draw", i)][:, :, cut], in_=rows[:, :, cut])
-
-        def loads(i):
-            return [(load_d, i, 0), (load_d, i, 1)] if i in SPLIT_LOAD else [(load_d, i, 2)]
-
-        def load_rho():
+        def load_rho_row():
             nc.sync.dma_start(out=rho_row[:], in_=rho.partition_broadcast(P))
 
+        def load_z(i):
+            h, j = divmod(i, PASSES)
+            raw = buffer(("z_raw", i), [P, SUBTILES, K_PASS], BF16, i % Z_BUFS)
+            part = z[h * W:(h + 1) * W, j * K_PASS:(j + 1) * K_PASS]
+            nc.sync.dma_start(out=raw[:], in_=part.rearrange("(a p) k -> p a k", p=P))
+
+        def z_bank(i, u):
+            return HIGH + (2 * i + u) % 4
+
         def turn_z(i, u):
-            tb = bank(4 + (2 * i + u) % 4)
-            tl[("zt", i, u)] = tb
-            for a in range(4):
-                words = tl[("zraw", i)][:, a, :].bitcast(F32)
-                nc.tensor.transpose(tb[:, a * P:(a + 1) * P], words[:, u:256:2], ident[:])
+            turned = bank(z_bank(i, u))
+            tiles[("z_t", i, u)] = turned
+            for a in range(SUBTILES):
+                words = tiles[("z_raw", i)][:, a, :].bitcast(F32)
+                nc.tensor.transpose(turned[:, a * P:(a + 1) * P], words[:, u:K_PASS // 2:2], ident[:])
 
         def relu_z(i, u):
             if u == 0:
-                stile(("ct", i), [P, PACK, W], BF16, i % CT_BUFS)
-            halves = tl[("zt", i, u)][:].bitcast(BF16)
+                buffer(("c_rows", i), [P, PACK, W], BF16, i % RELU_BUFS)
+            halves = tiles[("z_t", i, u)][:].bitcast(BF16)
             for e in range(2):
                 t = 2 * u + e
                 col = PACK * (i % PASSES) + t
-                nc.scalar.activation(out=tl[("ct", i)][:, t, :], in_=halves[:, e:2 * W:2], func=ACT.Relu,
-                                     bias=neg_bias[:, col:col + 1], scale=abs_g[:, col:col + 1])
+                nc.scalar.activation(out=tiles[("c_rows", i)][:, t, :], in_=halves[:, e:2 * W:2], func=ACT.Relu,
+                                     bias=relu_bias[:, col:col + 1], scale=abs_g[:, col:col + 1])
 
-        def weave_z(i):
-            dst = stile(("cg", i), [P, PACK * W], BF16, i % GROUP_BUFS)
-            nc.vector.tensor_copy(out=dst[:].rearrange("p (c i t) -> p c t i", i=4, t=PACK),
-                                  in_=tl[("ct", i)][:].rearrange("p t (c i) -> p c t i", i=4))
+        def weave_c(i):
+            woven = buffer(("c_woven", i), [P, PACK * W], BF16, i % WOVEN_BUFS["c"])
+            nc.vector.tensor_copy(out=woven[:].rearrange("p (m e t) -> p m t e", e=4, t=PACK),
+                                  in_=tiles[("c_rows", i)][:].rearrange("p t (m e) -> p m t e", e=4))
 
-        def quant(kind, i):
-            codes = stile((kind + "codes", i), [P, W], U32, i)
-            scales = stile((kind + "scales", i), [P, W], U8, i)
-            nc.vector.quantize_mx(out=codes[:].bitcast(FP8X4), scales=scales[:], in_=tl[(kind + "g", i)][:])
+        def load_d(i):
+            grp, j = divmod(i, PASSES)
+            raw = buffer(("d_raw", i), [P, PACK, W], BF16, i % D_BUFS)
+            part = D[j * K_PASS:(j + 1) * K_PASS, grp * W:(grp + 1) * W]
+            nc.sync.dma_start(out=raw[:], in_=part.rearrange("(p r) n -> p r n", r=PACK))
 
-        def sign(kind, i):
-            raw = tl[(kind, i)]
-            for j in range(PACK):
-                col = PACK * (i % PASSES) + j
-                nc.vector.tensor_scalar(out=raw[:, j, :], in0=raw[:, j, :], scalar1=sign_g[:, col:col + 1],
+        def sign_d(i):
+            raw = tiles[("d_raw", i)]
+            for r in range(PACK):
+                col = PACK * (i % PASSES) + r
+                nc.vector.tensor_scalar(out=raw[:, r, :], in0=raw[:, r, :], scalar1=sign_g[:, col:col + 1],
                                         scalar2=None, op0=ALU.mult)
 
         def weave_d(i, part):
-            if ("dg", i) not in tl:
-                stile(("dg", i), [P, PACK * W], BF16, i % (GROUP_BUFS + 1))
-            cut = (slice(0, 64), slice(64, 128), slice(0, 128))[part]
-            dst = tl[("dg", i)][:].rearrange("p (t m j) -> p m j t", t=4, j=PACK)[:, cut]
-            src = tl[("draw", i)][:].rearrange("p j (m t) -> p m j t", t=4)[:, cut]
-            if (i, part) in SCALAR_D:
+            if ("d_woven", i) not in tiles:
+                buffer(("d_woven", i), [P, PACK * W], BF16, i % WOVEN_BUFS["d"])
+            cut = (slice(0, P // 4), slice(P // 4, P // 2), slice(0, P // 2))[part]
+            dst = tiles[("d_woven", i)][:].rearrange("p (t m e r) -> p m t r e", t=PACK, e=2, r=PACK)[:, cut]
+            src = tiles[("d_raw", i)][:].rearrange("p r (m e t) -> p m t r e", e=2, t=PACK)[:, cut]
+            if (weave_d, i, part) in scalar:
                 nc.scalar.copy(out=dst, in_=src)
             else:
                 nc.vector.tensor_copy(out=dst, in_=src)
 
-        def weaves(i):
-            split = (i, 0) in SCALAR_D or (i, 1) in SCALAR_D
-            return [(weave_d, i, 0), (weave_d, i, 1)] if split else [(weave_d, i, 2)]
+        def quantize(operand, i):
+            nc.vector.quantize_mx(out=codes[operand][:, i, :].bitcast(FP8X4), scales=scales[operand][:, i, :],
+                                  in_=tiles[(operand + "_woven", i)][:])
 
-        def multiply(gi, h, lo, wd, k, t, bk):
-            if k == 0:
-                tl[("acc", gi, h, lo, t)] = bank(bk)
-            di, zi = gi * PASSES + k, h * PASSES + k
+        def multiply(grp, h, lo, width, t, j, bank_number):
+            if j == 0:
+                tiles[("sums", grp, h, lo, t)] = bank(bank_number)
+            d_unit, c_unit = grp * PASSES + j, h * PASSES + j
             nc.tensor.matmul_mx(
-                out=tl[("acc", gi, h, lo, t)][:, 0:wd],
-                lhsT=tl[("dcodes", di)][:, t * P:(t + 1) * P].bitcast(FP8X4),
-                lhsT_scale=tl[("dscales", di)][:, t * P:(t + 1) * P],
-                rhs=tl[("ccodes", zi)][:, lo:lo + wd].bitcast(FP8X4),
-                rhs_scale=tl[("cscales", zi)][:, lo:lo + wd],
-                start=(k == 0), stop=(k == PASSES - 1))
+                out=tiles[("sums", grp, h, lo, t)][:, 0:width],
+                lhsT=codes["d"][:, d_unit, t * P:(t + 1) * P].bitcast(FP8X4),
+                lhsT_scale=scales["d"][:, d_unit, t * P:(t + 1) * P],
+                rhs=codes["c"][:, c_unit, lo:lo + width].bitcast(FP8X4),
+                rhs_scale=scales["c"][:, c_unit, lo:lo + width],
+                start=(j == 0), stop=(j == PASSES - 1))
 
-        def drain(gi, h, lo, wd, t):
-            if ("w", gi, h) not in tl:
-                stile(("w", gi, h), [P, PACK, W], F32, 2 * gi + h)
-            col = PACK * gi + t
-            dst, src = tl[("w", gi, h)][:, t, lo:lo + wd], tl[("acc", gi, h, lo, t)][:, 0:wd]
-            bias, scale = sigma_b[:, col:col + 1], flat[:, 72 + col:73 + col]
-            if (gi, h, lo, t) in VECTOR_DRAIN:
-                nc.vector.tensor_scalar(out=dst, in0=src, scalar1=scale, scalar2=bias, op0=ALU.mult, op1=ALU.add)
-            else:
+        def drain(grp, h, lo, width, t):
+            if ("w", grp, h) not in tiles:
+                buffer(("w", grp, h), [P, PACK, W], F32, 2 * grp + h)
+            col = PACK * grp + t
+            dst, src = tiles[("w", grp, h)][:, t, lo:lo + width], tiles[("sums", grp, h, lo, t)][:, 0:width]
+            scale, bias = sigma_f[:, col:col + 1], sigma_b[:, col:col + 1]
+            if (drain, grp, h, lo, width, t) in scalar:
                 nc.scalar.activation(out=dst, in_=src, func=ACT.Identity, bias=bias, scale=scale)
-
-        def weave_y(gi, h, lo, wd):
-            dst = stile(("yg", gi, h, lo), [P, PACK * wd], BF16, pieces.index((gi, h, lo, wd)) % 2)
-            factor = rho_row[:, h * W + lo:h * W + lo + wd].rearrange("p (c i) -> p c i", i=4)
-            nc.vector.tensor_tensor(
-                out=dst[:].rearrange("p (c i t) -> p c t i", i=4, t=PACK),
-                in0=tl[("w", gi, h)][:, :, lo:lo + wd].rearrange("p t (c i) -> p c t i", i=4),
-                in1=factor.unsqueeze(2).to_broadcast([P, wd // 4, PACK, 4]), op=ALU.mult)
-
-        def quant_y(gi, h, lo, wd):
-            codes = stile(("ycodes", gi, h, lo), [P, wd], U32, pieces.index((gi, h, lo, wd)) % 2)
-            m0 = h * W + lo
-            nc.vector.quantize_mx(out=codes[:].bitcast(FP8X4), scales=y_scales[gi][:, m0:m0 + wd],
-                                  in_=tl[("yg", gi, h, lo)][:])
-
-        def store_words(gi, h, lo, wd):
-            m0 = h * W + lo
-            nc.sync.dma_start(out=out_1[gi, :, m0:m0 + wd, :].rearrange("p m t -> p (m t)").bitcast(I32),
-                              in_=tl[("ycodes", gi, h, lo)][:].bitcast(I32))
-
-        def store_scales(gi):
-            for q in range(4):
-                nc.sync.dma_start(out=out_2[gi, 4 * q:4 * q + 4, :].bitcast(I32),
-                                  in_=y_scales[gi][32 * q:32 * q + 4, :].bitcast(I32))
-
-        def turn_w(gi, h, a, bk):
-            tb = bank(bk)
-            tl[("wt", gi, h, a)] = tb
-            for t in range(PACK):
-                nc.tensor.transpose(tb[:, t * P:(t + 1) * P], tl[("w", gi, h)][:, t, a * P:(a + 1) * P], ident[:])
-
-        def finish(gi, h, a):
-            yo = stile(("yo", gi, h, a), [P, W], F32, (8 * gi + 4 * h + a) % OUT_BUFS)
-            dst = yo[:].rearrange("m (p t) -> m p t", t=PACK)
-            src = tl[("wt", gi, h, a)][:].rearrange("m (t p) -> m p t", t=PACK)
-            scale = rho_col[:, 4 * h + a:4 * h + a + 1]
-            if (gi, h, a) in VECTOR_FINISH:
-                nc.vector.tensor_scalar(out=dst, in0=src, scalar1=scale, scalar2=None, op0=ALU.mult)
             else:
-                nc.scalar.activation(out=dst, in_=src, func=ACT.Copy, scale=scale)
+                nc.vector.tensor_scalar(out=dst, in0=src, scalar1=scale, scalar2=bias, op0=ALU.mult, op1=ALU.add)
 
-        def store_y(gi, h, a):
-            m0 = h * W + a * P
-            nc.sync.dma_start(out=out_0[m0:m0 + P, gi * W:(gi + 1) * W], in_=tl[("yo", gi, h, a)][:])
+        def weave_y(n):
+            grp, h, lo, width = pieces[n]
+            woven = buffer(("y_woven", n), [P, PACK * width], BF16, n % PLANE_BUFS)
+            factor = rho_row[:, h * W + lo:h * W + lo + width].rearrange("p (m e) -> p m e", e=2)
+            nc.vector.tensor_tensor(
+                out=woven[:].rearrange("p (m e t) -> p m t e", e=2, t=PACK),
+                in0=tiles[("w", grp, h)][:, :, lo:lo + width].rearrange("p t (m e) -> p m t e", e=2),
+                in1=factor.unsqueeze(2).to_broadcast([P, width // 2, PACK, 2]), op=ALU.mult)
 
-        def covering(gi, h, lo, wd):
-            return [s for s in scalar + vector if s[0] is drain and s[1:3] == (gi, h) and s[3] < lo + wd and lo < s[3] + s[4]]
+        def quantize_y(n):
+            grp, h, lo, width = pieces[n]
+            y_codes = buffer(("y_codes", n), [P, width], U32, n % PLANE_BUFS)
+            nc.vector.quantize_mx(out=y_codes[:].bitcast(FP8X4), in_=tiles[("y_woven", n)][:],
+                                  scales=y_scales[grp][:, h * W + lo:h * W + lo + width])
 
-        def needs(step):
-            f, a = step[0], step[1:]
-            if f is load_z:
-                return [(turn_z, a[0] - RAW_BUFS, 1)] if a[0] >= RAW_BUFS else []
-            if f is load_d:
-                j = a[0] - D_BUFS
-                return weaves(j) if j >= 0 else []
-            if f is relu_constants:
-                return [(turn_constants,)]
-            if f is late_constants:
-                return [(turn_rho,), (relu_constants,)]
-            if f is turn_z:
-                return [(load_z, a[0])] + freed[step]
-            if f is relu_z:
-                return [(turn_z, a[0], a[1]), (relu_constants,)] + ([(weave_z, a[0] - CT_BUFS)] if a[0] >= CT_BUFS else [])
-            if f is weave_z:
-                r = [(sign, "ct", a[0])] if a[0] % PASSES in SIGN_ON_C else [(relu_z, a[0], 1)]
-                return r + ([(quant, "c", a[0] - GROUP_BUFS)] if a[0] >= GROUP_BUFS else [])
-            if f is sign:
-                return loads(a[1]) + [(relu_constants,)] if a[0] == "draw" else [(relu_z, a[1], 1)]
-            if f is weave_d:
-                j = a[0] - GROUP_BUFS - 1
-                r = [x for x in loads(a[0]) if 2 in (x[2], a[1]) or x[2] == a[1]] if a[0] % PASSES in SIGN_ON_C else [(sign, "draw", a[0])]
-                return r + ([(quant, "d", j)] if j >= 0 else [])
-            if f is quant:
-                if a[0] == "c":
-                    return [(weave_z, a[1])]
-                return weaves(a[1])
-            if f is multiply:
-                gi, h, lo, wd, k, t, bk = a
-                r = [(quant, "d", gi * PASSES + k), (quant, "c", h * PASSES + k)]
-                return r + (freed[step] if k == 0 else [(multiply, gi, h, lo, wd, k - 1, t, bk)])
-            if f is drain:
-                return [last_pass[a], (late_constants,)]
-            if f is weave_y:
-                n = pieces.index(a)
-                return covering(*a) + [(load_rho,)] + ([(quant_y,) + pieces[n - 2]] if n >= 2 else [])
-            if f is quant_y:
-                n = pieces.index(a)
-                return [(weave_y,) + a] + ([(store_words,) + pieces[n - 2]] if n >= 2 else [])
-            if f is store_words:
-                return [(quant_y,) + a]
-            if f is store_scales:
-                return [s for s in vector if s[0] is quant_y and s[1] == a[0]]
-            if f is turn_w:
-                gi, h, at, bk = a
-                return covering(gi, h, at * P, P) + freed[step]
-            if f is finish:
-                n = outs.index(a)
-                r = [s for s in tensor if s[0] is turn_w and s[1:4] == a]
-                return r + ([(store_y,) + outs[n - OUT_BUFS]] if n >= OUT_BUFS else [])
-            if f is store_y:
-                return [(finish,) + a]
-            return []
+        def store_words(n):
+            grp, h, lo, width = pieces[n]
+            dst = out_1[grp, :, h * W + lo:h * W + lo + width, :].rearrange("p m t -> p (m t)")
+            nc.sync.dma_start(out=dst.bitcast(I32), in_=tiles[("y_codes", n)][:].bitcast(I32))
 
-        H = W // 2
-        pieces = [(0, 0, 0, W), (0, 1, 0, W), (1, 0, 0, W)] + [(1, 1) + x for x in TAIL]
-        rest = range(STREAMED, 4)
-        groups = [(lo, wd, t) for lo, wd in TAIL for t in rest]
-        outs = [(gi, h, a) for gi in range(2) for h in range(2) for a in range(4)]
-        tensor, scalar, vector, sync = [], [], [], []
-        L = PASSES
+        def store_scales(grp):
+            for q in range(4):
+                nc.sync.dma_start(out=out_2[grp, 4 * q:4 * q + 4, :].bitcast(I32),
+                                  in_=y_scales[grp][32 * q:32 * q + 4, :].bitcast(I32))
 
-        def passes(gi, h, k, ts, first_bank):
-            return [(multiply, gi, h, 0, W, k, t, first_bank + t) for t in ts]
+        def turn_w(n, bank_number):
+            grp, h, a = out_tiles[n]
+            turned = bank(bank_number)
+            tiles[("w_t", n)] = turned
+            for t in range(PACK):
+                nc.tensor.transpose(turned[:, t * P:(t + 1) * P], tiles[("w", grp, h)][:, t, a * P:(a + 1) * P], ident[:])
 
-        def turns(n0, n1, banks):
-            return [(turn_w,) + outs[n] + (banks[n % len(banks)],) for n in range(n0, n1)]
+        def finish(n):
+            grp, h, a = out_tiles[n]
+            y = buffer(("y", n), [P, W], F32, n % OUT_BUFS)
+            col = SUBTILES * h + a
+            nc.scalar.activation(out=y[:].rearrange("m (p t) -> m p t", t=PACK),
+                                 in_=tiles[("w_t", n)][:].rearrange("m (t p) -> m p t", t=PACK),
+                                 func=ACT.Copy, scale=rho_col[:, col:col + 1])
 
-        def finishes(n0, n1):
-            return [(finish,) + outs[n] for n in range(n0, n1)]
+        def store_y(n):
+            grp, h, a = out_tiles[n]
+            first = h * W + a * P
+            nc.sync.dma_start(out=out_0[first:first + P, grp * W:(grp + 1) * W], in_=tiles[("y", n)][:])
 
-        def stores(n0, n1):
-            return [(store_y,) + outs[n] for n in range(n0, n1)]
+        pieces = [(0, 0, 0, W), (0, 1, 0, W), (1, 0, 0, W)] + [(1, 1) + piece for piece in PIECES_11]
+        out_tiles = [(grp, h, a) for grp in range(2) for h in range(2) for a in range(SUBTILES)]
+        last_groups = [(1, 1, lo, width, t) for lo, width in PIECES_11 for t in (2, 3)]
 
-        one = range(L)
+        def passes(grp, h, j, ts, first_bank):
+            return [(multiply, grp, h, 0, W, t, j, first_bank + t) for t in ts]
+
+        def last_group(n):
+            return [(multiply,) + last_groups[n] + (j, LOW + last_groups[n][4]) for j in range(PASSES)]
+
+        def drains(grp, h, ts):
+            return [(drain, grp, h, 0, W, t) for t in ts]
+
+        def last_drain(n):
+            return [(drain,) + last_groups[n]]
 
         def relus(i):
             return [(relu_z, i, 0), (relu_z, i, 1)]
 
-        def drains(gi, h, ts):
-            return [(drain, gi, h, 0, W, t) for t in ts]
+        def each(function, first, end):
+            return [(function, n) for n in range(first, end)]
 
-        def group(n):
-            lo, wd, t = groups[n]
-            return [(multiply, 1, 1, lo, wd, k, t, TAIL_BANKS[n % len(TAIL_BANKS)]) for k in one]
+        sync = [(load_z, 0), (load_d, 0)]
+        for j in range(1, PASSES):
+            sync += [(load_d, j), (load_z, j)]
+        for i in range(PASSES, UNITS):
+            sync += [(load_z, i), (load_d, i)]
+        sync += [(load_rho_row,)] + each(store_y, 0, 8) + each(store_words, 0, 2) + [(store_scales, 0)]
+        sync += each(store_y, 8, 11) + [(store_words, 2), (store_y, 11), (store_words, 3)] + each(store_y, 12, 14)
+        sync += [(store_words, 4)] + each(store_y, 14, 16) + [(store_words, 5), (store_scales, 1)]
 
-        def tail_drain(n):
-            return [(drain, 1, 1) + groups[n]]
-
-        def words(n):
-            return [(store_words,) + pieces[n]]
-
-        sync += [(load_z, 0)]
-        for k in range(L - 1):
-            sync += [(load_d, k, 2)] * (k == 0) + [(load_d, k + 1, 2), (load_z, k + 1)]
-        for k in one:
-            sync += [(load_z, L + k), (load_d, L + k, 2)]
-        sync += [(load_rho,)]
-        sync += stores(0, 8) + words(0) + words(1) + [(store_scales, 0)]
-        sync += stores(8, 10) + words(2) + stores(10, 13) + words(3) + stores(13, 16) + words(4) + [(store_scales, 1)]
-
-        tensor += [(turn_constants,), (turn_z, 0, 0), (turn_z, 0, 1), (turn_rho,)]
+        tensor = [(turn_vectors,), (turn_z, 0, 0), (turn_z, 0, 1), (turn_rho,)]
         tensor += [(turn_z, i, u) for i in range(1, LEAD) for u in range(2)]
-        ahead = [(turn_z, i, u) for i in range(LEAD, 2 * L) for u in range(2)]
-        for k in range(2 * L):
-            h, j = divmod(k, L)
-            early = ahead[0:EXTRA_TURN.count(k)]
-            ahead = ahead[len(early):]
-            if k >= RUNS_FROM:
-                tensor += early + passes(0, h, j, range(4), 0) + ahead[0:2]
+        ahead = [(turn_z, i, u) for i in range(LEAD, UNITS) for u in range(2)]
+        for i in range(UNITS):
+            h, j = divmod(i, PASSES)
+            if i in EXTRA_TURN:
+                tensor += ahead[0:1]
+                ahead = ahead[1:]
+            if h == 0:
+                tensor += passes(0, 0, j, (0, 1), LOW) + ahead[0:1] + passes(0, 0, j, (2, 3), LOW) + ahead[1:2]
             else:
-                tensor += early + passes(0, h, j, (0, 1), 0) + ahead[0:1] + passes(0, h, j, (2, 3), 0) + ahead[1:2]
+                tensor += passes(0, 1, j, range(PACK), LOW) + ahead[0:2]
             ahead = ahead[2:]
-            if k == L + FIRST_10:
-                tensor += passes(1, 0, 0, range(4), 4)
-        for k in one:
-            tensor += passes(1, 0, k, range(4), 4) if k > 0 else []
-            if k in TURNS:
-                n = 2 * TURNS.index(k)
-                tensor += turns(n, n + 2, (2, 3))
-            if k > 0:
-                tensor += passes(1, 1, k - 1, (0, 1), 0)
-        tensor += passes(1, 1, L - 1, (0, 1), 0)
-        tensor += group(0) + turns(8, 10, (4, 5)) + group(1) + turns(10, 12, (6, 7)) + group(2) + turns(12, 14, (0, 1))
-        tensor += group(3) + turns(14, 16, (4, 5))
+            if i == UNITS - 2:
+                tensor += passes(1, 0, 0, range(PACK), HIGH)
+        for j in range(1, PASSES):
+            tensor += passes(1, 0, j, range(PACK), HIGH)
+            if j in TURN_AFTER:
+                n = 2 * TURN_AFTER.index(j)
+                tensor += [(turn_w, n, LOW + 2), (turn_w, n + 1, LOW + 3)]
+            tensor += passes(1, 1, j - 1, (0, 1), LOW)
+        tensor += passes(1, 1, PASSES - 1, (0, 1), LOW)
+        tensor += last_group(0) + [(turn_w, 8, HIGH), (turn_w, 9, HIGH + 1)]
+        tensor += last_group(1) + [(turn_w, 10, HIGH + 2), (turn_w, 11, HIGH + 3)]
+        tensor += last_group(2) + last_group(3) + [(turn_w, 12, LOW), (turn_w, 13, LOW + 1), (turn_w, 14, HIGH)]
+        tensor += last_group(4) + last_group(5) + [(turn_w, 15, HIGH + 1)]
 
-        for k in one:
-            scalar += relus(k) + ([(weave_d, k + 1, 1)] if k + 1 < L else [])
-        second = [x for k in one for x in relus(L + k)]
-        scalar += second[:A_DRAIN] + drains(0, 0, (0, 1)) + second[A_DRAIN:]
-        scalar += [(weave_d, 9, 0), (weave_d, 9, 1), (weave_d, 10, 1)] + drains(0, 1, range(4))
-        scalar += [(weave_d, 11, 1)] + finishes(0, 1) + [(weave_d, 12, 1)] + finishes(1, 2) + [(weave_d, 13, 1)] + finishes(2, 4)
-        scalar += [(weave_d, 14, 1), (weave_d, 15, 1)] + finishes(4, 8)
-        scalar += drains(1, 0, range(4)) + drains(1, 1, (0,)) + finishes(8, 9) + tail_drain(0) + drains(1, 1, (1,)) + finishes(9, 10)
-        scalar += tail_drain(1) + finishes(10, 12) + tail_drain(2) + finishes(12, 14) + tail_drain(3) + finishes(14, 16)
+        scalar = relus(0) + [(weave_d, 0, SECOND)]
+        for j in range(1, PASSES):
+            scalar += [(weave_d, j, SECOND)] + relus(j)
+        scalar += relus(8) + relus(9) + drains(0, 0, (0, 1))
+        for i in range(10, UNITS):
+            scalar += relus(i)
+        scalar += [(weave_d, 9, FIRST), (weave_d, 9, SECOND), (weave_d, 10, SECOND)] + drains(0, 1, range(PACK))
+        scalar += [(weave_d, 11, SECOND), (weave_d, 12, SECOND)] + each(finish, 0, 2)
+        scalar += [(weave_d, 13, SECOND)] + each(finish, 2, 4)
+        scalar += [(weave_d, 14, SECOND), (weave_d, 15, SECOND)] + each(finish, 4, 8)
+        scalar += drains(1, 0, range(PACK)) + drains(1, 1, (0,)) + last_drain(0) + [(finish, 8)] + drains(1, 1, (1,))
+        scalar += [(finish, 9)] + last_drain(1) + each(finish, 10, 12) + last_drain(2) + last_drain(3)
+        scalar += each(finish, 12, 15) + last_drain(4) + last_drain(5) + [(finish, 15)]
 
-        vector += [(relu_constants,), (sign, "draw", 0), (weave_d, 0, 2), (sign, "draw", 1), (quant, "d", 0), (weave_d, 1, 0), (late_constants,)]
-        for k in range(L - 2):
-            vector += [(weave_z, k), (sign, "draw", k + 2), (quant, "c", k), (weave_d, k + 2, 0), (quant, "d", k + 1)]
-        vector += [(weave_z, L - 2), (quant, "d", L - 1), (quant, "c", L - 2), (weave_z, L - 1), (sign, "draw", L), (quant, "c", L - 1)]
-        fill = [x for x in drains(0, 0, range(4)) if x[1:4] + x[5:] in VECTOR_DRAIN]
-        vector += [[(weave_z, L)] + fill[0:1] + [(quant, "c", L)] + fill[1:2] + [(sign, "draw", 9)],
-                   [(weave_z, L), (sign, "draw", 9), (quant, "c", L)] + fill,
-                   [(weave_z, L)] + fill + [(quant, "c", L), (sign, "draw", 9)]][VORD]
-        vector += [(weave_z, 9), (weave_d, 8, 2), (quant, "c", 9), (weave_z, 10), (quant, "d", 8), (quant, "c", 10)]
-        vector += [(weave_z, 11), (weave_z, 12), (quant, "c", 11), (quant, "c", 12), (weave_z, 13), (quant, "c", 13)]
-        vector += [(weave_z, 14), (quant, "c", 14), (weave_z, 15), (sign, "draw", 10), (quant, "c", 15), (quant, "d", 9)]
-        for i in range(10, 2 * L - 1):
-            vector += [(weave_d, i, 0), (sign, "draw", i + 1), (quant, "d", i)]
-        vector += [(weave_d, 15, 0), (weave_y,) + pieces[0], (quant, "d", 15), (weave_y,) + pieces[1], (quant_y,) + pieces[0], (quant_y,) + pieces[1]]
-        for n in range(2, 5):
-            vector += [(weave_y,) + pieces[n], (quant_y,) + pieces[n]]
+        vector = [(relu_factors,), (sign_d, 0), (weave_d, 0, FIRST), (sign_d, 1), (weave_c, 0), (result_factors,)]
+        vector += [(weave_d, 1, FIRST), (quantize, "c", 0), (quantize, "d", 0)]
+        vector += [(sign_d, 2), (quantize, "d", 1), (weave_d, 2, FIRST)]
+        for j in range(1, PASSES - 2):
+            vector += [(weave_c, j), (sign_d, j + 2), (quantize, "c", j), (weave_d, j + 2, FIRST), (quantize, "d", j + 1)]
+        vector += [(weave_c, 6), (quantize, "d", 7), (quantize, "c", 6), (weave_c, 7), (sign_d, 8), (quantize, "c", 7)]
+        vector += [(weave_c, 8), (sign_d, 9), (quantize, "c", 8)] + drains(0, 0, (2, 3))
+        vector += [(weave_c, 9), (weave_d, 8, WHOLE), (quantize, "c", 9)]
+        vector += [(weave_c, 10), (quantize, "d", 8), (quantize, "c", 10)]
+        vector += [(weave_c, 11), (weave_c, 12), (quantize, "c", 11), (quantize, "c", 12)]
+        vector += [(weave_c, 13), (quantize, "c", 13), (weave_c, 14), (quantize, "c", 14)]
+        vector += [(weave_c, 15), (sign_d, 10), (quantize, "c", 15), (quantize, "d", 9)]
+        for i in range(10, UNITS - 1):
+            vector += [(weave_d, i, FIRST), (sign_d, i + 1), (quantize, "d", i)]
+        vector += [(weave_d, 15, FIRST), (weave_y, 0), (quantize, "d", 15), (weave_y, 1), (quantize_y, 0), (quantize_y, 1)]
+        for n in range(2, len(pieces)):
+            vector += [(weave_y, n), (quantize_y, n)]
 
-        freed, last_pass, holder = {}, {}, {0: (relu_constants,), 1: (late_constants,)}
-        for s in tensor:
-            if s[0] is turn_z:
-                bk = 4 + (2 * s[1] + s[2]) % 4
-                freed[s] = [holder[bk]] if bk in holder else []
-                holder[bk] = (relu_z, s[1], s[2])
-            elif s[0] is multiply:
-                if s[5] == 0:
-                    freed[s] = [holder[s[7]]] if s[7] in holder else []
-                    holder[s[7]] = (drain,) + s[1:5] + (s[6],)
-                last_pass[s[1:5] + (s[6],)] = s
-            elif s[0] is turn_w:
-                freed[s] = [holder[s[4]]]
-                holder[s[4]] = (finish,) + s[1:4]
+        last_reader = {LOW: (relu_factors,), LOW + 1: (result_factors,)}
+        bank_free = {}
+        for step in tensor:
+            if step[0] is turn_z:
+                taken, reader = z_bank(step[1], step[2]), (relu_z,) + step[1:]
+            elif step[0] is turn_w:
+                taken, reader = step[2], (finish, step[1])
+            elif step[0] is multiply and step[6] == 0:
+                taken, reader = step[7], (drain,) + step[1:6]
+            else:
+                continue
+            bank_free[step] = [last_reader[taken]] if taken in last_reader else []
+            last_reader[taken] = reader
 
-        head()
+        def among(queue, function, start):
+            return [s for s in queue if s[0] is function and s[1:1 + len(start)] == start]
+
+        def drains_over(grp, h, lo, width):
+            return [s for s in among(scalar + vector, drain, (grp, h)) if s[3] < lo + width and lo < s[3] + s[4]]
+
+        def earlier(function, n, bufs, *more):
+            return [(function, n - bufs) + more] if n >= bufs else []
+
+        def needs(step):
+            function, args = step[0], step[1:]
+            if function is relu_factors:
+                return [(turn_vectors,)]
+            if function is result_factors:
+                return [(turn_rho,), (relu_factors,)]
+            if function is load_z:
+                return earlier(turn_z, args[0], Z_BUFS, 1)
+            if function is turn_z:
+                return [(load_z, args[0])] + bank_free[step]
+            if function is relu_z:
+                return [(turn_z,) + args, (relu_factors,)] + earlier(weave_c, args[0], RELU_BUFS)
+            if function is weave_c:
+                return [(relu_z, args[0], 1)] + among(vector, quantize, ("c", args[0] - WOVEN_BUFS["c"]))
+            if function is load_d:
+                return among(scalar + vector, weave_d, (args[0] - D_BUFS,))
+            if function is sign_d:
+                return [(load_d, args[0]), (relu_factors,)]
+            if function is weave_d:
+                return [(sign_d, args[0])] + among(vector, quantize, ("d", args[0] - WOVEN_BUFS["d"]))
+            if function is quantize:
+                return [(weave_c, args[1])] if args[0] == "c" else among(scalar + vector, weave_d, (args[1],))
+            if function is multiply:
+                grp, h, j = args[0], args[1], args[5]
+                operands = [(quantize, "d", grp * PASSES + j), (quantize, "c", h * PASSES + j)]
+                return operands + bank_free.get(step, [])
+            if function is drain:
+                return among(tensor, multiply, args) + [(result_factors,)]
+            if function is weave_y:
+                return drains_over(*pieces[args[0]]) + [(load_rho_row,)] + earlier(quantize_y, args[0], PLANE_BUFS)
+            if function is quantize_y:
+                return [(weave_y, args[0])] + earlier(store_words, args[0], PLANE_BUFS)
+            if function is store_words:
+                return [(quantize_y, args[0])]
+            if function is store_scales:
+                return [(quantize_y, n) for n in range(len(pieces)) if pieces[n][0] == args[0]]
+            if function is turn_w:
+                grp, h, a = out_tiles[args[0]]
+                return drains_over(grp, h, a * P, P) + bank_free[step]
+            if function is finish:
+                return among(tensor, turn_w, args) + earlier(store_y, args[0], OUT_BUFS)
+            if function is store_y:
+                return [(finish, args[0])]
+            return []
+
+        stage_vectors()
         written = set()
         queues = [sync, tensor, scalar, vector]
-        places = [0, 0, 0, 0]
-        while any(places[e] < len(queues[e]) for e in range(4)):
-            moved = False
-            for e in range(4):
-                while places[e] < len(queues[e]) and all(s in written for s in needs(queues[e][places[e]])):
-                    step = queues[e][places[e]]
+        places = [0] * len(queues)
+        while len(written) < sum(len(queue) for queue in queues):
+            before = len(written)
+            for engine, queue in enumerate(queues):
+                while places[engine] < len(queue) and all(s in written for s in needs(queue[places[engine]])):
+                    step = queue[places[engine]]
                     step[0](*step[1:])
                     written.add(step)
-                    places[e] += 1
-                    moved = True
-            assert moved
+                    places[engine] += 1
+            assert len(written) > before, "the four orders wait for each other"

from contextlib import ExitStack

import concourse.mybir as mybir
from concourse.masks import make_identity

M, K, N = 1024, 4096, 1024
FLOPS = 2 * M * K * N

F32 = mybir.dt.float32
BF16 = mybir.dt.bfloat16
U32 = mybir.dt.uint32
I32 = mybir.dt.int32
U8 = mybir.dt.uint8
FP8X4 = mybir.dt.float8_e4m3fn_x4
ALU = mybir.AluOpType
ACT = mybir.ActivationFunctionType

P = 128
PACK = 4
K_PASS = P * PACK
PASSES = K // K_PASS
UNITS = 2 * PASSES
W = 512
SUBTILES = W // P

Z_BUFS = 6
D_BUFS = 8
RELU_BUFS = 3
WOVEN_BUFS = {"c": 2, "d": 3}
PLANE_BUFS = 2
OUT_BUFS = 4

THETA_ROW, G_ROW, B_ROW, SIGMA_ROW, RHO_ROW = 0, 8, 16, 18, 20

FIRST, SECOND, WHOLE = 0, 1, 2

LOW, HIGH = 0, 4
LEAD = 3
EXTRA_TURN = (6, 9)
TURN_AFTER = (2, 3, 5, 6)
PIECES_11 = ((0, 256), (256, 128), (384, 128))


def tile_dictionary_relu_readout_g1_kernel(tc, z, theta, g, D, b, sigma, rho, out_0, out_1, out_2):
    nc = tc.nc
    with ExitStack() as ctx:
        sb = ctx.enter_context(tc.tile_pool(name="sb", bufs=1))
        ps = ctx.enter_context(tc.psum_pool(name="ps", bufs=1))
        ctx.enter_context(tc.manual_schedule())
        tiles = {}

        def bank(bank_number, dtype=F32, width=W):
            name = "bank%d" % bank_number
            return ps.tile([P, width], dtype, name=name, tag=name)

        def buffer(key, shape, dtype, slot):
            name = "%s%d" % (key[0], slot)
            tiles[key] = sb.tile(shape, dtype, name=name, tag=name, align_bytes=64)
            return tiles[key]

        ident = sb.tile([P, P], F32, name="ident")
        ident_bf = sb.tile([P, P], BF16, name="ident_bf")
        stage = sb.tile([P, W], BF16, name="stage")
        vectors = sb.tile([P, RHO_ROW * PACK], F32, name="vectors")
        theta_k = vectors[:, PACK * THETA_ROW:PACK * G_ROW]
        g_k = vectors[:, PACK * G_ROW:PACK * B_ROW]
        b_f = vectors[:, PACK * B_ROW:PACK * SIGMA_ROW]
        sigma_f = vectors[:, PACK * SIGMA_ROW:PACK * RHO_ROW]
        abs_g = sb.tile([P, PACK * PASSES], F32, name="abs_g")
        relu_bias = sb.tile([P, PACK * PASSES], F32, name="relu_bias")
        sign_g = sb.tile([P, PACK * PASSES], F32, name="sign_g")
        sigma_b = sb.tile([P, 2 * PACK], F32, name="sigma_b")
        rho_col = sb.tile([P, M // P], F32, name="rho_col")
        rho_row = sb.tile([P, M], BF16, name="rho_row")
        codes = {"c": sb.tile([P, UNITS, W], U32, name="c_codes", align_bytes=256),
                 "d": sb.tile([P, UNITS, W], U32, name="d_codes", align_bytes=256)}
        scales = {"c": sb.tile([P, UNITS, W], U8, name="c_scales", align_bytes=256),
                  "d": sb.tile([P, UNITS, W], U8, name="d_scales", align_bytes=256)}
        y_scales = [sb.tile([P, M], U8, name="y_scales%d" % grp, align_bytes=64) for grp in range(2)]

        def stage_vectors():
            nc.vector.memset(stage[:].bitcast(U32), 0)
            for row, vec, width in ((THETA_ROW, theta, W), (G_ROW, g, W), (B_ROW, b, W), (SIGMA_ROW, sigma, W),
                                    (RHO_ROW, rho, P)):
                rows = vec.rearrange("(r c) -> r c", c=width)
                nc.scalar.dma_start(out=stage[row:row + rows.shape[0], 0:width], in_=rows)
            make_identity(nc, ident[:])
            nc.scalar.activation(out=ident_bf[:], in_=ident[:], func=ACT.Relu)

        def turn_vectors():
            tiles["vectors_t"] = bank(LOW)
            words = stage[:].bitcast(F32)
            for u in range(2):
                nc.tensor.transpose(tiles["vectors_t"][:, u * P:(u + 1) * P], words[:, u:W // 2:2], ident[:])

        def turn_rho():
            tiles["rho_t"] = bank(LOW + 1, BF16, 2 * W)
            nc.tensor.transpose(tiles["rho_t"][:, 0:P], stage[:, 0:P], ident_bf[:])

        def relu_factors():
            halves = tiles["vectors_t"][:].bitcast(BF16)[:, 0:4 * P].rearrange("p (u r e) -> p r u e", u=2, e=2)
            nc.vector.tensor_copy(out=vectors[:].rearrange("p (r u e) -> p r u e", u=2, e=2),
                                  in_=halves[:, 0:RHO_ROW, :, :])
            nc.vector.scalar_tensor_tensor(out=abs_g[:], in0=g_k, scalar=-1.0, in1=g_k, op0=ALU.mult, op1=ALU.max)
            nc.vector.tensor_scalar(out=sign_g[:], in0=g_k, scalar1=0.0, scalar2=2.0, op0=ALU.is_ge, op1=ALU.mult)
            nc.vector.scalar_tensor_tensor(out=relu_bias[:], in0=theta_k, scalar=-1.0, in1=abs_g[:],
                                           op0=ALU.mult, op1=ALU.mult)
            nc.vector.tensor_scalar(out=sign_g[:], in0=sign_g[:], scalar1=-1.0, scalar2=None, op0=ALU.add)

        def result_factors():
            nc.vector.tensor_tensor(out=sigma_b[:], in0=b_f, in1=sigma_f, op=ALU.mult)
            nc.vector.tensor_copy(out=rho_col[:], in_=tiles["rho_t"][:, RHO_ROW:RHO_ROW + M // P])

        def load_rho_row():
            nc.sync.dma_start(out=rho_row[:], in_=rho.partition_broadcast(P))

        def load_z(i):
            h, j = divmod(i, PASSES)
            raw = buffer(("z_raw", i), [P, SUBTILES, K_PASS], BF16, i % Z_BUFS)
            part = z[h * W:(h + 1) * W, j * K_PASS:(j + 1) * K_PASS]
            nc.sync.dma_start(out=raw[:], in_=part.rearrange("(a p) k -> p a k", p=P))

        def z_bank(i, u):
            return HIGH + (2 * i + u) % 4

        def turn_z(i, u):
            turned = bank(z_bank(i, u))
            tiles[("z_t", i, u)] = turned
            for a in range(SUBTILES):
                words = tiles[("z_raw", i)][:, a, :].bitcast(F32)
                nc.tensor.transpose(turned[:, a * P:(a + 1) * P], words[:, u:K_PASS // 2:2], ident[:])

        def relu_z(i, u):
            if u == 0:
                buffer(("c_rows", i), [P, PACK, W], BF16, i % RELU_BUFS)
            halves = tiles[("z_t", i, u)][:].bitcast(BF16)
            for e in range(2):
                t = 2 * u + e
                col = PACK * (i % PASSES) + t
                nc.scalar.activation(out=tiles[("c_rows", i)][:, t, :], in_=halves[:, e:2 * W:2], func=ACT.Relu,
                                     bias=relu_bias[:, col:col + 1], scale=abs_g[:, col:col + 1])

        def weave_c(i):
            woven = buffer(("c_woven", i), [P, PACK * W], BF16, i % WOVEN_BUFS["c"])
            nc.vector.tensor_copy(out=woven[:].rearrange("p (m e t) -> p m t e", e=4, t=PACK),
                                  in_=tiles[("c_rows", i)][:].rearrange("p t (m e) -> p m t e", e=4))

        def load_d(i):
            grp, j = divmod(i, PASSES)
            raw = buffer(("d_raw", i), [P, PACK, W], BF16, i % D_BUFS)
            part = D[j * K_PASS:(j + 1) * K_PASS, grp * W:(grp + 1) * W]
            nc.sync.dma_start(out=raw[:], in_=part.rearrange("(p r) n -> p r n", r=PACK))

        def sign_d(i):
            raw = tiles[("d_raw", i)]
            for r in range(PACK):
                col = PACK * (i % PASSES) + r
                nc.vector.tensor_scalar(out=raw[:, r, :], in0=raw[:, r, :], scalar1=sign_g[:, col:col + 1],
                                        scalar2=None, op0=ALU.mult)

        def weave_d(i, part):
            if ("d_woven", i) not in tiles:
                buffer(("d_woven", i), [P, PACK * W], BF16, i % WOVEN_BUFS["d"])
            cut = (slice(0, P // 4), slice(P // 4, P // 2), slice(0, P // 2))[part]
            dst = tiles[("d_woven", i)][:].rearrange("p (t m e r) -> p m t r e", t=PACK, e=2, r=PACK)[:, cut]
            src = tiles[("d_raw", i)][:].rearrange("p r (m e t) -> p m t r e", e=2, t=PACK)[:, cut]
            if (weave_d, i, part) in scalar:
                nc.scalar.copy(out=dst, in_=src)
            else:
                nc.vector.tensor_copy(out=dst, in_=src)

        def quantize(operand, i):
            nc.vector.quantize_mx(out=codes[operand][:, i, :].bitcast(FP8X4), scales=scales[operand][:, i, :],
                                  in_=tiles[(operand + "_woven", i)][:])

        def multiply(grp, h, lo, width, t, j, bank_number):
            if j == 0:
                tiles[("sums", grp, h, lo, t)] = bank(bank_number)
            d_unit, c_unit = grp * PASSES + j, h * PASSES + j
            nc.tensor.matmul_mx(
                out=tiles[("sums", grp, h, lo, t)][:, 0:width],
                lhsT=codes["d"][:, d_unit, t * P:(t + 1) * P].bitcast(FP8X4),
                lhsT_scale=scales["d"][:, d_unit, t * P:(t + 1) * P],
                rhs=codes["c"][:, c_unit, lo:lo + width].bitcast(FP8X4),
                rhs_scale=scales["c"][:, c_unit, lo:lo + width],
                start=(j == 0), stop=(j == PASSES - 1))

        def drain(grp, h, lo, width, t):
            if ("w", grp, h) not in tiles:
                buffer(("w", grp, h), [P, PACK, W], F32, 2 * grp + h)
            col = PACK * grp + t
            dst, src = tiles[("w", grp, h)][:, t, lo:lo + width], tiles[("sums", grp, h, lo, t)][:, 0:width]
            scale, bias = sigma_f[:, col:col + 1], sigma_b[:, col:col + 1]
            if (drain, grp, h, lo, width, t) in scalar:
                nc.scalar.activation(out=dst, in_=src, func=ACT.Identity, bias=bias, scale=scale)
            else:
                nc.vector.tensor_scalar(out=dst, in0=src, scalar1=scale, scalar2=bias, op0=ALU.mult, op1=ALU.add)

        def weave_y(n):
            grp, h, lo, width = pieces[n]
            woven = buffer(("y_woven", n), [P, PACK * width], BF16, n % PLANE_BUFS)
            factor = rho_row[:, h * W + lo:h * W + lo + width].rearrange("p (m e) -> p m e", e=2)
            nc.vector.tensor_tensor(
                out=woven[:].rearrange("p (m e t) -> p m t e", e=2, t=PACK),
                in0=tiles[("w", grp, h)][:, :, lo:lo + width].rearrange("p t (m e) -> p m t e", e=2),
                in1=factor.unsqueeze(2).to_broadcast([P, width // 2, PACK, 2]), op=ALU.mult)

        def quantize_y(n):
            grp, h, lo, width = pieces[n]
            y_codes = buffer(("y_codes", n), [P, width], U32, n % PLANE_BUFS)
            nc.vector.quantize_mx(out=y_codes[:].bitcast(FP8X4), in_=tiles[("y_woven", n)][:],
                                  scales=y_scales[grp][:, h * W + lo:h * W + lo + width])

        def store_words(n):
            grp, h, lo, width = pieces[n]
            dst = out_1[grp, :, h * W + lo:h * W + lo + width, :].rearrange("p m t -> p (m t)")
            nc.sync.dma_start(out=dst.bitcast(I32), in_=tiles[("y_codes", n)][:].bitcast(I32))

        def store_scales(grp):
            for q in range(4):
                nc.sync.dma_start(out=out_2[grp, 4 * q:4 * q + 4, :].bitcast(I32),
                                  in_=y_scales[grp][32 * q:32 * q + 4, :].bitcast(I32))

        def turn_w(n, bank_number):
            grp, h, a = out_tiles[n]
            turned = bank(bank_number)
            tiles[("w_t", n)] = turned
            for t in range(PACK):
                nc.tensor.transpose(turned[:, t * P:(t + 1) * P], tiles[("w", grp, h)][:, t, a * P:(a + 1) * P], ident[:])

        def finish(n):
            grp, h, a = out_tiles[n]
            y = buffer(("y", n), [P, W], F32, n % OUT_BUFS)
            col = SUBTILES * h + a
            nc.scalar.activation(out=y[:].rearrange("m (p t) -> m p t", t=PACK),
                                 in_=tiles[("w_t", n)][:].rearrange("m (t p) -> m p t", t=PACK),
                                 func=ACT.Copy, scale=rho_col[:, col:col + 1])

        def store_y(n):
            grp, h, a = out_tiles[n]
            first = h * W + a * P
            nc.sync.dma_start(out=out_0[first:first + P, grp * W:(grp + 1) * W], in_=tiles[("y", n)][:])

        pieces = [(0, 0, 0, W), (0, 1, 0, W), (1, 0, 0, W)] + [(1, 1) + piece for piece in PIECES_11]
        out_tiles = [(grp, h, a) for grp in range(2) for h in range(2) for a in range(SUBTILES)]
        last_groups = [(1, 1, lo, width, t) for lo, width in PIECES_11 for t in (2, 3)]

        def passes(grp, h, j, ts, first_bank):
            return [(multiply, grp, h, 0, W, t, j, first_bank + t) for t in ts]

        def last_group(n):
            return [(multiply,) + last_groups[n] + (j, LOW + last_groups[n][4]) for j in range(PASSES)]

        def drains(grp, h, ts):
            return [(drain, grp, h, 0, W, t) for t in ts]

        def last_drain(n):
            return [(drain,) + last_groups[n]]

        def relus(i):
            return [(relu_z, i, 0), (relu_z, i, 1)]

        def each(function, first, end):
            return [(function, n) for n in range(first, end)]

        sync = [(load_z, 0), (load_d, 0)]
        for j in range(1, PASSES):
            sync += [(load_d, j), (load_z, j)]
        for i in range(PASSES, UNITS):
            sync += [(load_z, i), (load_d, i)]
        sync += [(load_rho_row,)] + each(store_y, 0, 8) + each(store_words, 0, 2) + [(store_scales, 0)]
        sync += each(store_y, 8, 11) + [(store_words, 2), (store_y, 11), (store_words, 3)] + each(store_y, 12, 14)
        sync += [(store_words, 4)] + each(store_y, 14, 16) + [(store_words, 5), (store_scales, 1)]

        tensor = [(turn_vectors,), (turn_z, 0, 0), (turn_z, 0, 1), (turn_rho,)]
        tensor += [(turn_z, i, u) for i in range(1, LEAD) for u in range(2)]
        ahead = [(turn_z, i, u) for i in range(LEAD, UNITS) for u in range(2)]
        for i in range(UNITS):
            h, j = divmod(i, PASSES)
            if i in EXTRA_TURN:
                tensor += ahead[0:1]
                ahead = ahead[1:]
            if h == 0:
                tensor += passes(0, 0, j, (0, 1), LOW) + ahead[0:1] + passes(0, 0, j, (2, 3), LOW) + ahead[1:2]
            else:
                tensor += passes(0, 1, j, range(PACK), LOW) + ahead[0:2]
            ahead = ahead[2:]
            if i == UNITS - 2:
                tensor += passes(1, 0, 0, range(PACK), HIGH)
        for j in range(1, PASSES):
            tensor += passes(1, 0, j, range(PACK), HIGH)
            if j in TURN_AFTER:
                n = 2 * TURN_AFTER.index(j)
                tensor += [(turn_w, n, LOW + 2), (turn_w, n + 1, LOW + 3)]
            tensor += passes(1, 1, j - 1, (0, 1), LOW)
        tensor += passes(1, 1, PASSES - 1, (0, 1), LOW)
        tensor += last_group(0) + [(turn_w, 8, HIGH), (turn_w, 9, HIGH + 1)]
        tensor += last_group(1) + [(turn_w, 10, HIGH + 2), (turn_w, 11, HIGH + 3)]
        tensor += last_group(2) + last_group(3) + [(turn_w, 12, LOW), (turn_w, 13, LOW + 1), (turn_w, 14, HIGH)]
        tensor += last_group(4) + last_group(5) + [(turn_w, 15, HIGH + 1)]

        scalar = relus(0) + [(weave_d, 0, SECOND)]
        for j in range(1, PASSES):
            scalar += [(weave_d, j, SECOND)] + relus(j)
        scalar += relus(8) + relus(9) + drains(0, 0, (0, 1))
        for i in range(10, UNITS):
            scalar += relus(i)
        scalar += [(weave_d, 9, FIRST), (weave_d, 9, SECOND), (weave_d, 10, SECOND)] + drains(0, 1, range(PACK))
        scalar += [(weave_d, 11, SECOND), (weave_d, 12, SECOND)] + each(finish, 0, 2)
        scalar += [(weave_d, 13, SECOND)] + each(finish, 2, 4)
        scalar += [(weave_d, 14, SECOND), (weave_d, 15, SECOND)] + each(finish, 4, 8)
        scalar += drains(1, 0, range(PACK)) + drains(1, 1, (0,)) + last_drain(0) + [(finish, 8)] + drains(1, 1, (1,))
        scalar += [(finish, 9)] + last_drain(1) + each(finish, 10, 12) + last_drain(2) + last_drain(3)
        scalar += each(finish, 12, 15) + last_drain(4) + last_drain(5) + [(finish, 15)]

        vector = [(relu_factors,), (sign_d, 0), (weave_d, 0, FIRST), (sign_d, 1), (weave_c, 0), (result_factors,)]
        vector += [(weave_d, 1, FIRST), (quantize, "c", 0), (quantize, "d", 0)]
        vector += [(sign_d, 2), (quantize, "d", 1), (weave_d, 2, FIRST)]
        for j in range(1, PASSES - 2):
            vector += [(weave_c, j), (sign_d, j + 2), (quantize, "c", j), (weave_d, j + 2, FIRST), (quantize, "d", j + 1)]
        vector += [(weave_c, 6), (quantize, "d", 7), (quantize, "c", 6), (weave_c, 7), (sign_d, 8), (quantize, "c", 7)]
        vector += [(weave_c, 8), (sign_d, 9), (quantize, "c", 8)] + drains(0, 0, (2, 3))
        vector += [(weave_c, 9), (weave_d, 8, WHOLE), (quantize, "c", 9)]
        vector += [(weave_c, 10), (quantize, "d", 8), (quantize, "c", 10)]
        vector += [(weave_c, 11), (weave_c, 12), (quantize, "c", 11), (quantize, "c", 12)]
        vector += [(weave_c, 13), (quantize, "c", 13), (weave_c, 14), (quantize, "c", 14)]
        vector += [(weave_c, 15), (sign_d, 10), (quantize, "c", 15), (quantize, "d", 9)]
        for i in range(10, UNITS - 1):
            vector += [(weave_d, i, FIRST), (sign_d, i + 1), (quantize, "d", i)]
        vector += [(weave_d, 15, FIRST), (weave_y, 0), (quantize, "d", 15), (weave_y, 1), (quantize_y, 0), (quantize_y, 1)]
        for n in range(2, len(pieces)):
            vector += [(weave_y, n), (quantize_y, n)]

        last_reader = {LOW: (relu_factors,), LOW + 1: (result_factors,)}
        bank_free = {}
        for step in tensor:
            if step[0] is turn_z:
                taken, reader = z_bank(step[1], step[2]), (relu_z,) + step[1:]
            elif step[0] is turn_w:
                taken, reader = step[2], (finish, step[1])
            elif step[0] is multiply and step[6] == 0:
                taken, reader = step[7], (drain,) + step[1:6]
            else:
                continue
            bank_free[step] = [last_reader[taken]] if taken in last_reader else []
            last_reader[taken] = reader

        def among(queue, function, start):
            return [s for s in queue if s[0] is function and s[1:1 + len(start)] == start]

        def drains_over(grp, h, lo, width):
            return [s for s in among(scalar + vector, drain, (grp, h)) if s[3] < lo + width and lo < s[3] + s[4]]

        def earlier(function, n, bufs, *more):
            return [(function, n - bufs) + more] if n >= bufs else []

        def needs(step):
            function, args = step[0], step[1:]
            if function is relu_factors:
                return [(turn_vectors,)]
            if function is result_factors:
                return [(turn_rho,), (relu_factors,)]
            if function is load_z:
                return earlier(turn_z, args[0], Z_BUFS, 1)
            if function is turn_z:
                return [(load_z, args[0])] + bank_free[step]
            if function is relu_z:
                return [(turn_z,) + args, (relu_factors,)] + earlier(weave_c, args[0], RELU_BUFS)
            if function is weave_c:
                return [(relu_z, args[0], 1)] + among(vector, quantize, ("c", args[0] - WOVEN_BUFS["c"]))
            if function is load_d:
                return among(scalar + vector, weave_d, (args[0] - D_BUFS,))
            if function is sign_d:
                return [(load_d, args[0]), (relu_factors,)]
            if function is weave_d:
                return [(sign_d, args[0])] + among(vector, quantize, ("d", args[0] - WOVEN_BUFS["d"]))
            if function is quantize:
                return [(weave_c, args[1])] if args[0] == "c" else among(scalar + vector, weave_d, (args[1],))
            if function is multiply:
                grp, h, j = args[0], args[1], args[5]
                operands = [(quantize, "d", grp * PASSES + j), (quantize, "c", h * PASSES + j)]
                return operands + bank_free.get(step, [])
            if function is drain:
                return among(tensor, multiply, args) + [(result_factors,)]
            if function is weave_y:
                return drains_over(*pieces[args[0]]) + [(load_rho_row,)] + earlier(quantize_y, args[0], PLANE_BUFS)
            if function is quantize_y:
                return [(weave_y, args[0])] + earlier(store_words, args[0], PLANE_BUFS)
            if function is store_words:
                return [(quantize_y, args[0])]
            if function is store_scales:
                return [(quantize_y, n) for n in range(len(pieces)) if pieces[n][0] == args[0]]
            if function is turn_w:
                grp, h, a = out_tiles[args[0]]
                return drains_over(grp, h, a * P, P) + bank_free[step]
            if function is finish:
                return among(tensor, turn_w, args) + earlier(store_y, args[0], OUT_BUFS)
            if function is store_y:
                return [(finish, args[0])]
            return []

        stage_vectors()
        written = set()
        queues = [sync, tensor, scalar, vector]
        places = [0] * len(queues)
        while len(written) < sum(len(queue) for queue in queues):
            before = len(written)
            for engine, queue in enumerate(queues):
                while places[engine] < len(queue) and all(s in written for s in needs(queue[places[engine]])):
                    step = queue[places[engine]]
                    step[0](*step[1:])
                    written.add(step)
                    places[engine] += 1
            assert len(written) > before, "the four orders wait for each other"
